import numpy as np, ml_dtypes
CORES = [8,136,40,168]
N = 4
BF = ml_dtypes.bfloat16
C, WS, WE, CAP, RO = 256, 4096, 1024, 48, 4
M, H = 16 * C, 8 * C
PL = np.arange(16)[:, None]
def tables(rng):
    amp = rng.choice(np.array([30, 100, 255]), (N, 8, 1, 1))
    e = np.floor((2 * rng.random((N, 8, 16, WS)) - 1) * amp).astype(np.int64)
    return np.clip(rng.integers(0, 256, (N, 8, 1, WS)) + e, 0, 255), rng.integers(0, 64, (N, 8, 16, WE)), rng.integers(0, 16, (N, 8, 16, 2))
def still(rng):
    return rng.integers(0, 41, (N, 8, 16, WS)), rng.integers(41, 64, (N, 8, 16, WE)), rng.integers(0, 16, (N, 8, 16, 2))
def chains(rng, K, keys, td):
    L = np.full((N, 8, 16, C), -1, np.int64); n = np.zeros((N, 8, C), np.int64)
    for g in range(8):
        low = [rng.permutation(H)[:int(K[g, r])] for r in range(N)]
        for r in range(N):
            lo = low[r]; hi = rng.permutation(low[(r - 1) % N]) + H
            o = np.argsort(keys[r, g].reshape(-1))[:len(lo) + len(hi) - 4 * C]
            m = 4 + np.bincount(o // 12, minlength=C)
            c0 = np.flatnonzero(td[r, g] == 0); c1 = np.flatnonzero(td[r, g] == 1)
            A = np.full((16, C), -1, np.int64)
            A[m[c0] - 1, c0] = lo[:len(c0)]; A[m[c1] - 1, c1] = hi[:len(c1)]
            A[(PL < m) & (A < 0)] = rng.permutation(np.concatenate([lo[len(c0):], hi[len(c1):]]))
            L[r, g] = A; n[r, g] = m
    return L, n
def monos(rng, n, low):
    z = rng.integers(0, 64, (N, 8, 16, C)); t = np.where(low, rng.integers(0, 8, low.shape), rng.integers(8, 64, low.shape))
    return np.where(PL == n[:, :, None, :] - 1, t[:, :, None, :], z)
def pack(tb, L, n, z):
    z = np.where(PL < n[:, :, None, :], z, 0); b = [np.ascontiguousarray(v.reshape(N, 128, -1)).astype(np.float32).astype(BF) for v in tb]
    return {"spr": b[0], "bar": b[1], "wt": b[2], "lam": np.ascontiguousarray(L.reshape(N, 128, C)).astype(np.int32), "mon": np.ascontiguousarray(z.reshape(N, 128, C)).astype(np.int32), "cnt": n.astype(np.int32)}
def anyway():
    return np.full((N, 8, C), -1)
def bring(A, v, k, c):
    i, j = np.nonzero(A == v); i, j = int(i[0]), int(j[0])
    A[i, j] = A[k, c]; A[k, c] = v
def crowd(rng, spr, wt, L, n, z):
    spr[:, 4, 0] = rng.integers(0, 256, (N, WS)); spr[:, 4, 1] = 32
    wt[:, 4] = 0; wt[:, 4, 0, 0] = 1; wt[:, 4, 1, 1] = 1
    for r in range(0, N, 2):
        A, A1 = L[r, 4], L[r + 1, 4]; v = int(np.min(A[A >= 0])); A1[A1 == v + H] = H; A[A == v] = 0
    tails = {}
    for s in range(1, N, 2):
        A = L[s, 4]; x = rng.permutation(A[A >= 0]); x = rng.permutation(x[np.unique(x >> 3, return_index=True)[1]])
        lo = x[x < H][:CAP]; hi = np.concatenate([np.array([H]), x[(x >= H) & ((x >> 3) != C)]])[:CAP]; tails[s] = (lo, hi)
        for v, c in zip(np.concatenate([lo, hi]), rng.permutation(C)):
            k = int(n[s, 4, c]) - 1; bring(L[s, 4], v, k, c); z[s, 4, k, c] = 0
    for r in range(0, N, 2):
        s0, s1 = (r - 1) % N, r + 1; lo, hi = tails[s0][0], tails[s1][1]
        o = 1 + rng.permutation(C - 2); a = np.concatenate([np.array([C - 1]), o[:2 * CAP - 1]]); q = np.insert(o[2 * CAP - 1:4 * CAP - 2], CAP, 0)
        for m, v in enumerate(np.concatenate([lo + H, hi - H])):
            bring(L[r, 4], v, 15 if m == 0 else int(rng.integers(0, n[r, 4, a[m]])), a[m])
        spr[s0, 4, 0, lo >> 3] = q[:CAP]; spr[s1, 4, 0, hi >> 3] = q[CAP:]; spr[s1, 4, :, C] = 0
def setup_inputs(rng):
    L, n = chains(rng, rng.integers(3 * C, 6 * C + 1, (8, N)), rng.random((N, 8, C, 12)) + 0.4 * rng.random((N, 8, C, 1)), anyway())
    low = rng.random((N, 8, C)) < rng.choice(np.array([0.1, 0.3, 0.5, 0.8]), (N, 8, 1))
    return pack(tables(rng), L, n, monos(rng, n, low))
def setup_inputs_room(rng):
    ch = np.array([0, 1, CAP - 1, CAP, CAP + 1, C // 2]); td = anyway(); low = np.zeros((N, 8, C), bool)
    for r in range(N):
        for g in range(8):
            a, b = int(rng.choice(ch)), int(rng.choice(ch))
            if r == 0: a, b = (CAP, CAP + 1, CAP - 1, 1, 0, C // 2, CAP, CAP + 1)[g], (CAP + 1, CAP, C // 2, 0, 1, CAP - 1, CAP + 1, CAP)[g]
            o = rng.permutation(C); td[r, g, o[:a]] = 0; td[r, g, o[a:a + b]] = 1; low[r, g, o[:a + b]] = True
    L, n = chains(rng, rng.integers(3 * C, 6 * C + 1, (8, N)), rng.random((N, 8, C, 12)), td)
    return pack(still(rng), L, n, monos(rng, n, low))
def setup_inputs_ties(rng):
    spr, bar, wt = tables(rng)
    for r in range(N):
        for g in range(8):
            P = int(rng.choice(np.array([4, 16, 64])))
            if r == 0: P = (4, 16, 64, 4, 16, 64, 16, 4)[g]
            top = np.argsort(np.argsort(rng.random((16, P)), axis=0), axis=0) < rng.integers(7, 11, (1, P))
            pat = rng.integers(0, 101, (16, 1)) + np.where(top, rng.choice(np.array([20, 21, 40]), (1, P)), 0)
            pat[:, 0] = pat[:, 0] - np.where(top[:, 0], pat[:, 0] - np.min(pat, axis=1), 0)
            spr[r, g] = pat[:, np.where(rng.random(WS) < 0.4, 0, rng.integers(0, P, WS))]
    bar = np.broadcast_to(rng.choice(np.array([0, 19, 20, 21, 40]), (N, 8, 1, WE)), bar.shape)
    L, n = chains(rng, rng.integers(3 * C, 6 * C + 1, (8, N)), rng.random((N, 8, C, 12)), anyway())
    return pack((spr, bar, wt), L, n, rng.choice(np.array([0, 1, 7, 8, 9, 15, 16, 56, 60, 63]), (N, 8, 16, C)))
def setup_inputs_clash(rng):
    spr, bar, wt = still(rng); wt[:, :3, :, 0] = 0; wt[:, 3] = 0; wt[:, 3, 0] = 1; wt[:, 3, 1] = rng.integers(0, 3, (N, 2))
    spr[::2, 5] = rng.integers(0, 2, (N // 2, 16, WS)); spr[1::2, 5] = rng.integers(245, 256, (N // 2, 16, WS))
    wt[1::2, 5, :, 0] = np.where(np.arange(16) < 12, 15, 10); wt[1::2, 5, 0, 1] = 15
    keys = rng.random((N, 8, C, 12)) + 2 * rng.integers(0, 2, (N, 8, C, 1))
    keys[:, 0:3:2, 0, :6] = -1; keys[:, 0:3:2, 0, 6:] = 9; keys[:, 1, 0] = -1
    keys[:, 4:6] = rng.random((N, 2, C, 12)); keys[:, 4:6, :, 0] = -1; keys[:, 4:6, :, 11] = 9
    keys[::2, 4, C - 1] = -1
    L, n = chains(rng, rng.integers(3 * C, 6 * C + 1, (8, N)), keys, anyway())
    for r in range(N):
        kk, cc = np.nonzero(L[r, 0] >= H); i = int(rng.integers(0, len(kk))); v = int(L[r, 0, kk[i], cc[i]])
        L[r, 0, kk[i], cc[i]] = L[r, 0, 0, 0]; L[r, 0, 0, 0] = v
    for r in range(N):
        v = int(L[(r + 1) % N, 0, 0, 0]) - H; kk, cc = np.nonzero(L[r, 0] == v); t = int(n[r, 0, 1]) - 1
        L[r, 0, kk[0], cc[0]] = L[r, 0, t, 1]; L[r, 0, t, 1] = v
    low = rng.random((N, 8, C)) < 0.3; low[:, :3, 0] = False; low[:, :3, 1] = True
    low[:, 4] = False; low[::2, 5] = False; low[1::2, 5] = rng.random((N // 2, C)) < 0.5
    z = monos(rng, n, low); crowd(rng, spr, wt, L, n, z)
    return pack((spr, bar, wt), L, n, z)
def setup_inputs_full(rng):
    K = rng.integers(2 * C, 8 * C + 1, (8, N)); o = rng.permutation(8)
    K[o[0]] = 8 * C; K[o[1]] = 2 * C; K[o[2]] = np.where(np.arange(N) % 2 == 0, 2 * C, 8 * C)
    L, n = chains(rng, K, rng.random((N, 8, C, 12)), anyway())
    low = rng.random((N, 8, C)) < rng.choice(np.array([0.0, 0.05, 0.2, 1.0]), (N, 8, 1))
    return pack(tables(rng), L, n, monos(rng, n, low))
def setup_inputs_spread(rng):
    spr = np.minimum(np.exp2(8 * rng.random((N, 8, 1, WS))) * (0.25 + rng.random((N, 8, 16, WS))), 255).astype(np.int64)
    bar = (np.exp2(6 * rng.random((N, 8, 16, WE))) - 1).astype(np.int64); wt = (np.exp2(4 * rng.random((N, 8, 16, 2))) - 1).astype(np.int64)
    L, n = chains(rng, rng.integers(2 * C, 8 * C + 1, (8, N)), rng.random((N, 8, C, 12)) + 1.5 * rng.random((N, 8, C, 1)), anyway())
    z = np.where(rng.random((N, 8, 1, C)) < 0.5, (64 * rng.random((N, 8, 16, C)) ** 4).astype(np.int64), 63 - (64 * rng.random((N, 8, 16, C)) ** 4).astype(np.int64))
    return pack((spr, bar, wt), L, n, z)
def check_inputs(d):
    bad = []
    for k, lo, hi in (("spr", 0, 255), ("bar", 0, 63), ("wt", 0, 15), ("lam", -1, M - 1), ("mon", 0, 63), ("cnt", 4, 16)):
        v = np.asarray(d[k]).astype(np.float64)
        if not np.all((v >= lo) & (v <= hi) & (v == np.floor(v))): bad.append("range of " + k)
    L = np.asarray(d["lam"]).astype(np.int64).reshape(N, 8, 16, C); z = np.asarray(d["mon"]).reshape(N, 8, 16, C); ok = PL < np.asarray(d["cnt"])[:, :, None, :]
    if np.any((L >= 0) != ok) or np.any((L != -1) & ~ok): bad.append("places of lam")
    if np.any((z != 0) & ~ok): bad.append("empty places of mon")
    have = np.zeros((N, 8, M), np.int64); r, g, k, c = np.nonzero(ok); np.add.at(have, (r, g, np.clip(L[r, g, k, c], 0, M - 1)), 1)
    if np.any(have > 1): bad.append("a name stands twice")
    if np.any(have[:, :, :H] != np.roll(have[:, :, H:], -1, axis=0)): bad.append("twins")
    return bad
def reference(spr, bar, wt, lam, mon, cnt):
    S, B, w = [v.astype(np.float32).astype(np.int64).reshape(N, 8, 16, -1) for v in (spr, bar, wt)]
    L = lam.astype(np.int64).reshape(N, 8, 16, C); z = mon.astype(np.int64).reshape(N, 8, 16, C); n = cnt.astype(np.int64)
    for t in range(RO):
        ok = PL < n[:, :, None, :]; x = np.where(ok, L, 0)
        i = ((((x + 77 * t) & (M - 1)) * (2 * z + 1)) >> 3) & (WS - 1)
        j = (((x[:, :, 1:] * (z[:, :, :-1] + 64)) >> 5) + 811 * z[:, :, 1:]) & (WE - 1)
        F = np.take_along_axis(S, i.reshape(N, 8, 1, 16 * C), 3).reshape(N, 8, 16, 16, C)
        E = np.take_along_axis(B, j.reshape(N, 8, 1, 15 * C), 3).reshape(N, 8, 16, 15, C)
        D = F[:, :, :, 1:] - F[:, :, :, :-1]
        up = np.add.reduce((D > E).astype(np.int64), axis=2) >= 9; down = np.add.reduce((-D > E).astype(np.int64), axis=2) >= 9
        s = np.zeros((N, 8, 17, C), np.int64); s[:, :, 1:16] = np.where(ok[:, :, 1:], 8 * up.astype(np.int64) - 8 * down.astype(np.int64), 0)
        z = np.where(ok, np.clip(z + s[:, :, :16] - s[:, :, 1:], 0, 63), 0)
        last = n - 1; zl = np.take_along_axis(z, last[:, :, None, :], 2)[:, :, 0]; ll = np.take_along_axis(L, last[:, :, None, :], 2)[:, :, 0]
        f = np.take_along_axis(F, last[:, :, None, None, :], 3)[:, :, :, 0]
        u1 = np.add.reduce(w[..., 0:1] * f, axis=2); u2 = np.add.reduce(w[..., 1:2] * f, axis=2)
        qn = (((u1 & 4095) * (u2 & 4095)) >> 5) & (C - 1)
        ev = [(zl < 8) & (ll < H), (zl < 8) & (ll >= H)]
        ev = [e & (np.add.accumulate(e.astype(np.int64), axis=2) <= CAP) for e in ev]
        sends = ev[0] | ev[1]
        moved = np.zeros((N, 8, C), bool); src = np.broadcast_to(PL, L.shape).copy(); grow = np.zeros((N, 8, C), np.int64); put = []
        for r in range(N):
            for g in range(8):
                p0, p1 = (r - 1) % N, (r + 1) % N
                a0 = np.flatnonzero(ev[0][p0, g]); a1 = np.flatnonzero(ev[1][p1, g])
                home = np.concatenate([np.full(len(a0), p0), np.full(len(a1), p1)]); hc = np.concatenate([a0, a1])
                name = np.concatenate([ll[p0, g, a0] + H, ll[p1, g, a1] - H]); q = qn[home, g, hc]; fm = f[home, g, :, hc].T
                kk, cc = np.nonzero(ok[r, g]); inv = np.zeros(M, np.int64); inv[L[r, g, kk, cc]] = 16 * cc + kk
                a = inv[name] >> 4; p = inv[name] & 15; m = np.arange(len(a))
                first = np.full(C, len(a)); np.minimum.at(first, a, m); np.minimum.at(first, q, m)
                good = (n[r, g, a] > 4) & (a != q) & (n[r, g, q] < 16) & ~sends[r, g, a] & ~sends[r, g, q] & (first[a] == m) & (first[q] == m)
                a, p, q, name, fm, home, hc = a[good], p[good], q[good], name[good], fm[:, good], home[good], hc[good]
                dist = np.add.reduce(np.abs(F[r, g][:, :, q] - fm[:, None, :]), axis=0)
                b = np.argmin(np.where(PL < n[r, g, q], dist, 2 ** 20), axis=0)
                moved[home, g, hc] = True
                src[r, g][:, a] = PL + (PL >= p); src[r, g][:, q] = PL - (PL > b)
                grow[r, g, a] = -1; grow[r, g, q] = 1; put.append((r, g, b, q, name))
        src = np.minimum(np.where(moved[:, :, None, :], np.where(PL == 0, last[:, :, None, :], PL - 1), src), 15)
        L = np.take_along_axis(L, src, 2); z = np.take_along_axis(z, src, 2)
        z[:, :, 0] = np.where(moved, 16, z[:, :, 0])
        for r, g, b, q, name in put:
            L[r, g, b, q] = name; z[r, g, b, q] = 16
        n = n + grow; ok = PL < n[:, :, None, :]; L = np.where(ok, L, -1); z = np.where(ok, z, 0)
    return {"yl": L.reshape(N, 128, C).astype(np.float32), "yz": z.reshape(N, 128, C).astype(np.float32), "yn": n.astype(np.float32)}

from concourse.bass import DstId, RemoteDMATransfer
from concourse.mybir import AluOpType as AL, AxisListType, ActivationFunctionType as AF

F32, BF, I32, U16 = "float32", "bfloat16", "int32", "uint16"
RO = 4
BIG = 2.0 ** 95
ALPHA = 15.0 / 256
STEP = 2.0 ** -24
MODE = ("AAAAAAAA", "AAAAAABB")
_S = {
    F32: dict(W=464, rt=1024, inv=8408, val=4096, iU=264, iM=96, cs=12, ta=256, tb=256, ty=256, p1=256, wf=2, tw=264,
              Tt=528, thr=192, wr=96, dN=96, rB=96, dum=32, mc=4, acc=8, m1=384, l1=384, sN=96, sA=96, sT=96, gA=96,
              CC=192, CS=96, CT=96, OF=32, bd=32, of2=32, clF=8, t6=8, kb=96, KP=192, PP=192, XX=192, XS=96, Nq=96, Ns=96, q32=96,
              I32=128, nI32=128, B32=128, UmI=128, Dn32=128, nDn32=128, nDq=128, E0=128, yl_=256, yz_=256, yn_=256, sB=96),
    BF: dict(sp=4096, ba=1024, wts=2, F=4128, D=4096, Wt=4096, Fq=1536, Ab=1536, va=264, nv=256, th=264, pA=256, pQ=256, sg=256, ng=256,
             zb=256, up=256, dn=256, ind=256, dl=256, dh=256, cl_=264, ch_=264, jk=264, jl=264, r1=256, r2=256, iB=264, i16=256, c7=256,
             c16=256, cE=256, c48=256, dg=96, r0=96, fT=96, m2=768, l2=768, gd=384, la=384, i256=96, qd=96, sQ=96, a1=8, oh=3072, lt=192,
             eq=96, ge=96, bad=96, mT=192, mk=192, ww=96, t16=16, Fa=264,
             I=128, nI=128, I16=128, BI=128, nBI=128, Up=128, Dn=128, IU=128, nDS=128, Z=144, Zs=144, B1=128, TRI=128, D64=128, M0=128,
             M1=128, M2=128, M3=128, W1=128, W2=128, Z0=128, I5=128, n2k=128, one=128),
    I32: dict(lm=256, mo=256, Wi=256, xm=256, z2=256, P=256, y=264, ib=256, ri=256, ui=192, qi=96, pi=2, t2=2),
    U16: dict(oF=256, oB=256, oI=256, U=24, cU=8, sU=8, tU=16, fU=24, oQ=96, eL=2, aL=6),
    "float16": dict(M=2048),
}
_P = dict(pd=2048, p4=512, p5=512, p6=512, p7=512)
SCRATCH = {n + "_b": ("psum", [128, w], F32) for n, w in _P.items()}
_W = {n: (n + "_b", 0, w) for n, w in _P.items()}
for _dt, _d in _S.items():
    _o = 0
    for _n, _w in _d.items():
        _W[_n] = ("s_" + _dt, _o, _w)
        _o += (_w + 15) // 16 * 16
    SCRATCH["s_" + _dt] = ("sbuf", [128, _o], _dt)
SEMAPHORES = (["eV", "eS", "eP", "eG", "loc"] + ["d%d" % i for i in range(8)] + ["r%d" % i for i in range(3 * RO)])


def rank_program(g, core, T, topo):
    rank = T.rank_of(core)
    if rank is None:
        return
    N = len(T.cores)
    nxt, prv = T.cores[(rank + 1) % N], T.cores[(rank - 1) % N]
    Q = {"V": g.vector, "S": g.scalar, "P": g.tensor, "G": g, "Y": g.sync}
    ops = []

    def R(n, lo=0, hi=None, st=1, rows=None):
        b, o, w = _W[n]
        hi = w if hi is None else hi
        t = T[b]
        ap = t[:, o + lo:o + hi:st] if st != 1 else (t[0:rows, o + lo:o + hi] if rows else t[:, o + lo:o + hi])
        if n in _P:
            return ap, [(n, lo // 512 * 512, (hi + 511) // 512 * 512)]
        return ap, [(n, lo, hi)]

    def C(i):
        return R("cs", i, i + 1)

    def X(win, off):
        return win[0].indirect(off[0]), win[1] + off[1]

    def add(e, fn, out, ins, sem=None):
        rd = [r for a in ins if isinstance(a, tuple) for r in a[1]]
        wr = []
        for o in out:
            wr += o[1][:1]
            rd += o[1][1:]
        ops.append((e, fn, rd, wr, sem))

    def a_(x):
        return x[0] if isinstance(x, tuple) else x

    def ts(o, i, s1, o0, s2=None, o1=None):
        if o1 is None:
            add("V", lambda: g.vector.tensor_scalar(o[0], i[0], a_(s1), None, o0), [o], [i, s1])
        else:
            add("V", lambda: g.vector.tensor_scalar(o[0], i[0], a_(s1), a_(s2), o0, o1), [o], [i, s1, s2])

    def tt(o, a, b, op):
        add("V", lambda: g.vector.tensor_tensor(o[0], a[0], b[0], op), [o], [a, b])

    def cp(o, i):
        add("V", lambda: g.vector.tensor_copy(o[0], i[0]), [o], [i])

    def ms(o, v):
        add("V", lambda: g.vector.memset(o[0], v), [o], [])

    def sc(o, a, b, init, o0, o1):
        add("V", lambda: g.vector.tensor_tensor_scan(o[0], a[0], b[0], init, o0, o1), [o], [a, b])

    def tr(o, i):
        add("V", lambda: g.vector.transpose(o[0], i[0]), [o], [i])

    def act(o, i, f, bias=None, scale=None, acc=None):
        kw = {}
        if bias is not None:
            kw["bias"] = a_(bias)
        if scale is not None:
            kw["scale"] = a_(scale)
        if acc is not None:
            kw["accum_out"] = acc[0]
        add("S", lambda: g.scalar.activation(o[0], i[0], f, **kw), [o] + ([acc] if acc else []), [i, bias, scale])

    def mm(o, l, r, st=True, sp=True):
        add("P", lambda: g.tensor.matmul(o[0], l[0], r[0], st, sp), [o], [l, r])

    def mg(o, prs):
        for i, (l, r) in enumerate(prs):
            mm(o, R(l), r, i == 0, i == len(prs) - 1)

    def io(o, pat, base, cm, fl=True):
        kw = {"allow_small_or_imprecise_dtypes": True} if fl else {}
        add("G", lambda: g.iota(o[0], pat, base, cm, **kw), [o], [])

    def sel(o, i, pat, op, base, cm):
        add("G", lambda: g.affine_select(o[0], i[0], pat, op, 0.0, base, cm), [o], [i])

    nd = [0]

    def dma(e, o, i):
        s = "d%d" % nd[0]
        nd[0] += 1
        add(e, lambda: Q[e].dma_start(a_(o), a_(i)), [o] if isinstance(o, tuple) else [], [i], (s, 16))

    nloc = [0]

    def send(src, dst, b, w, sem, back=False):
        trs = []
        for h, to in enumerate((prv, nxt) if back else (nxt, prv)):
            en = topo.engines(core, to)
            en = en[h * len(en) // 2:(h + 1) * len(en) // 2]
            rid, pid = topo.addr(to, core)
            trs.append(RemoteDMATransfer(dst_ids=[DstId(rid=rid, pnc=pid)], dma_engine_mask=sum(1 << e for e in en), remote_sem=T.sem[sem],
                                         src=R(src, b + h * w, b + h * w + w)[0], dst=R(dst, b + h * w, b + h * w + w)[0]))
            nloc[0] += len(en)
        add("G", lambda: g.remote_dma_fused(trs, local_sem=T.sem.loc), [], [R(src, b, b + 2 * w)], ("", 0))
        got = sum(len(topo.engines(c, core)) // 2 for c in (nxt, prv))
        ops.append(("X", None, [], R(dst, b, b + 2 * w)[1], (sem, got)))

    A, SU, MU, MX, MN = AL.add, AL.subtract, AL.mult, AL.max, AL.min
    EQ, GE, GT, LT = AL.is_equal, AL.is_ge, AL.is_gt, AL.is_lt
    SH, AN = AL.arith_shift_right, AL.bitwise_and
    ID, SG, RL, CO = AF.Identity, AF.Sign, AF.Relu, AF.Copy

    dma("Y", R("lm"), T.lam[:])
    dma("Y", R("mo"), T.mon[:])
    dma("S", R("ba"), T.bar[:])
    dma("Y", R("sp"), T.spr[:])
    dma("Y", R("wts"), T.wt[:])
    for n, lo, hi, v in (("one", 0, 128, 1.0), ("sN", 0, 96, 0.25), ("sA", 0, 96, 0.0), ("c16", 0, 256, 15.875), ("cE", 0, 256, -31.0 / 1024),
                         ("Tt", 256, 264, BIG), ("Tt", 520, 528, BIG), ("y", 256, 264, 0), ("inv", 4096, 4104, 291.0)):
        ms(R(n, lo, hi), v)
    io(R("pi"), [[0, 2]], 0, 1, False)
    io(R("cs", 0, 2), [[12279, 2]], -12279, 1)
    io(R("iM"), [[0, 6], [1, 16]], 0, 0)
    sel(R("I"), R("one"), [[-1, 128]], EQ, 0, 1)
    io(R("iU"), [[1, 264]], 0, 0)
    sel(R("TRI"), R("one"), [[-16, 8], [0, 16]], GE, 0, 1)
    sel(R("B1"), R("TRI"), [[16, 8], [0, 16]], GE, 15, -1)
    sel(R("Up"), R("B1"), [[-1, 128]], EQ, -1, 1)
    sel(R("Dn"), R("B1"), [[-1, 128]], EQ, 1, 1)
    io(R("val", 0, 1024), [[1, 64], [0, 16]], 32, 0)
    io(R("F", 0, 16), [[0, 16]], 0, 0)
    io(R("sB", 0, 6), [[16, 6]], 15, 0)
    io(R("val", 1024, 2048), [[1, 64], [0, 16]], 96, 0)
    sel(R("TRI"), R("B1"), [[1, 128]], GE, 0, -1)
    for n, lo, hi, v in (("F", 4112, 4128, 0), ("c7", 0, 256, 7), ("c48", 0, 256, 48), ("W", 256, 264, 0),
                         ("va", 256, 264, 0), ("cl_", 0, 8, 0), ("ch_", 0, 8, 0), ("jk", 256, 264, -32), ("jl", 256, 264, -32),
                         ("tw", 256, 264, 4096), ("Fa", 256, 264, 0), ("th", 256, 264, 0), ("dum", 18, 32, 0), ("OF", 18, 32, 0), ("Z0", 0, 128, 0)):
        io(R(n, lo, hi), [[0, hi - lo]], v, 0)
    for h in range(2, 4):
        io(R("val", 1024 * h, 1024 * h + 1024), [[1, 64], [0, 16]], 32 + 64 * h, 0)
    ts(R("t2"), R("pi"), 15, AN)
    sc(R("wr"), R("sN"), R("sA"), 2.0 ** 94, MU, A)
    cp(C(3), R("t2", 0, 1))
    ts(R("r0"), R("iM"), 0.0, GT)
    tt(C(4), C(1), C(3), SU)
    ts(C(8), C(3), 1.0, A)
    ts(R("dg"), R("iM"), C(3), EQ)
    ts(C(9), C(3), 15.0, LT, 8192.0, MU)
    ts(C(10), C(3), 0.0, EQ)
    ts(C(4), C(4), 15.0, A)
    ts(R("sN"), R("iM"), C(3), EQ, 65536.0, MU)
    ts(R("sA"), R("iM"), C(8), EQ, -8192.0, MU)
    tt(R("sT"), R("wr"), R("dg"), MU)
    tt(R("dN"), R("sN"), R("sA"), A)
    sc(R("ww"), R("r0"), R("sT"), 0.0, MU, A)
    ts(R("t6", 0, 2), R("iU", 0, 32, 16), C(3), A)
    ts(R("Z"), R("iU", 0, 144), C(4), EQ)
    ts(R("t2"), R("t6", 0, 2), 1.0 / 6, MU, -0.4, A)
    ts(R("mc", 0, 3), R("iU", 0, 48, 16), C(3), A, 0.5, A)
    ts(R("t6", 2, 4), R("t2"), -6.0, MU)
    for j, b in enumerate((264.0, 360.0, 4104.0)):
        ts(R("dum", 6 * j, 6 * j + 6), R("iU", 0, 96, 16), C(3), A, b, A)
    tt(R("t6", 4, 6), R("t6", 0, 2), R("t6", 2, 4), A)
    ts(R("t16"), R("iU", 0, 256, 16), C(3), A, 16.0, MU)

    def scaled(l):
        for o, i, s in l:
            act(R(o), R(i), ID, None, s)

    act(R("thr", 0, 96), R("wr"), ID, None, 1.85)
    act(R("thr", 96, 192), R("wr"), ID, None, 1.85)
    act(R("rB"), R("r0"), ID, 65536.0, -65536.0)
    act(C(11), C(3), ID, None, 1.0 / 16)
    scaled((("nI", "I", -1.0), ("M0", "I", -106.5), ("I16", "I", 16.0), ("I5", "I", 512.0), ("BI", "I", BIG), ("nBI", "I", -BIG),
            ("I32", "I", 1.0), ("nI32", "I", -1.0), ("n2k", "I", -2048.0), ("E0", "I", C(10))))
    act(R("i16"), R("iU", 0, 256), ID, None, 16.0)
    act(R("iB"), R("iU"), CO)
    scaled((("D64", "Dn", 1.0 / 64), ("B32", "B1", 1.0), ("Zs", "Z", 1.0 / STEP), ("Dn32", "Dn", 1.0), ("nDn32", "Dn", -1.0),
            ("nDq", "Dn", -1.0 / 256)))

    def piece(h):
        return X(R("inv"), R("oI", 32 * h, 32 * h + 32)), R("val", 512 * h, 512 * h + 512)

    def silu(hs):
        for h in hs:
            o, i = piece(h)
            act(o, i, AF.Silu)

    W, va, y = R("W", 0, 256), R("va", 0, 256), R("y", 0, 256)
    lo4, lo5, hi5 = R("p4", 0, 256), R("p5", 0, 256), R("p5", 256, 512)
    lo6, hi6, lo7, hi7 = R("p6", 0, 256), R("p6", 256, 512), R("p7", 0, 256), R("p7", 256, 512)
    Wg, Fw, tpw = R("W", 0, 264), R("F", 16, 4128), R("p7", 0, 16)
    for t in range(RO):
        o7 = 77.0 * t
        last = t == RO - 1
        if t:
            ts(R("Wi"), W, 128.0 * (o7 - 1) + 1, A)
        else:
            ts(R("ta"), R("lm"), 128.0, MU, 127.0, A)
            ts(R("z2"), R("mo"), 2.0, MU, 1.0, A)
            tt(R("IU"), R("I"), R("Up"), SU)
            tt(W, R("ta"), R("z2"), A)
            ts(R("eL"), R("t6", 4, 6), 16.0, MU, 15.0, A)
        act(va, W, SG)
        mg(lo6, [("IU", va)])
        mg(hi6, [("B1", va)])
        if t:
            ts(R("xm"), R("Wi"), 7, SH, 4095, AN)
            ts(R("z2"), R("Wi"), 127, AN)
        else:
            ts(R("xm"), R("lm"), 4095, AN)
            cp(y, R("lm"))
        act(R("nv"), va, ID, 32.0, -32.0)
        if t == 0:
            mg(lo4, [("I5", R("nv")), ("I", R("i16"))])
            act(R("tb"), lo4, RL, C(0))
            act(R("rt", 0, 704), R("ba", 320, 1024), ID, 1.0 / STEP, 2.0 / STEP)
            act(R("rt", 704, 1024), R("ba", 0, 320), ID, 1.0 / STEP, 2.0 / STEP)
        act(R("th", 0, 256), lo6, ID, None, 256.0)
        tt(R("P"), R("xm"), R("z2"), MU)
        act(R("pA"), hi6, RL, 5 * BIG, -BIG)
        act(R("pQ"), hi6, RL, -15 * BIG, BIG)
        ts(R("xm"), R("P"), 3, SH, 4095, AN)
        ts(R("zb"), R("z2"), 127.0, A)
        cp(R("oF"), R("xm"))
        if t:
            cp(R("F", 16, 528), X(R("sp"), R("oF", 0, 32)))
            ts(y, R("Wi"), 7, SH)
        else:
            tt(R("ta"), R("tb"), y, A)
        mg(lo5, [("D64", R("zb"))])
        mg(hi5, [("M0", R("zb")), ("B1", R("cE"))] + ([("M%d" % t, R("zb"))] if t else []))
        if t == 0:
            cp(R("oI"), R("ta"))
            silu((0, 1))
            add("V", lambda: g.vector.reciprocal(R("rt")[0], R("rt")[0]), [R("rt")], [R("rt")])
            cp(R("wf"), R("wts"))
            cp(R("aL"), R("sB", 0, 6))
        tt(R("p1"), lo5, y, MU)
        tt(R("ty"), lo6, y, MU)
        tt(R("ib"), hi5, R("p1"), A)
        ts(R("P"), R("ib"), 1023, AN)
        cp(R("oB"), R("P"))

        def pc(n, i, w=4096):
            return R(n, 512 * i % w, 512 * i % w + 512)

        def gF(i):
            u = 512 * i
            if i or not t:
                act(R("F", 16 + u, 528 + u), X(R("sp"), R("oF", 32 * i, 32 * i + 32)), CO)
            mg(pc("pd", i, 2048), [("I", R("F", 16 + u, 528 + u)), ("nI", R("F", 15 + u, 527 + u))])

        def mid(i):
            rg = X(R("rt"), R("oB", 32 * i, 32 * i + 32))
            if MODE[t > 0][i] == "A":
                act(pc("D", i), pc("pd", i, 2048), CO)
                tt(pc("M", i, 2048), rg, pc("D", i), MU)
            else:
                act(pc("D", i), rg, CO)
                tt(pc("M", i, 2048), pc("pd", i, 2048), pc("D", i), MU)

        def cnt(a, b):
            o = R("p4", a // 16, b // 16)
            mm(o, R("I16"), R("va", a // 16, b // 16), True, False)
            for k in range(1, 16):
                mm(o, R("Zs", 15 - k, 143 - k), R("Wt", a + k, b, 16), False, k == 15)

        if t == 0:
            for h in (2, 3):
                cp(*piece(h))
        gF(0)
        gF(1)
        for i in range(9):
            if i < 6:
                gF(i + 2)
            if i < 8:
                mid(i)
            if i == 0:
                for j in range(16):
                    mm(tpw, R("Z", 15 - j, 143 - j), R("va", j, 256, 16), j == 0, False)
                mm(tpw, R("I"), R("t16"), False, True)
            if i == 1:
                mg(hi7, [("B32", R("ty"))])
            if i:
                ts(pc("Wt", i - 1), pc("M", i - 1, 2048), -ALPHA * STEP, MX, STEP, MN)
            if i == 2:
                ts(R("tU"), tpw, -1.0, A)
            if i == 5:
                cnt(0, 2048)
            if i == 6:
                cnt(2048, 3072)
        cnt(3072, 4096)
        act(R("sg"), hi7, SG, -2047.5 - o7)
        act(R("ng"), hi7, SG, 2047.5 + o7, -1.0)
        act(R("Fa", 0, 256), X(Fw, R("tU")), CO)
        if t == 0:
            scaled((("nDS", "IU", -16.0), ("UmI", "IU", -1.0), ("W1", "B1", R("wf", 0, 1)), ("W2", "B1", R("wf", 1, 2))))
            silu((4, 5))
        tt(R("ri"), lo4, R("nv"), A)
        mg(hi7, [("B32", R("ty")), ("n2k", R("sg"))])
        act(R("tw", 0, 256), hi7, ID, -o7)
        ts(R("up"), lo4, 24.4, GT, 16.0, MU)
        tt(R("dn"), lo4, R("ri"), GT)
        mg(lo5, [("I", R("zb")), ("B1", R("c7")), ("IU", R("up")), ("nDS", R("dn"))])
        tt(R("ind"), lo5, R("th", 0, 256), LT)
        mg(lo6, [("I", R("ng")), ("B1", R("ind"))])
        mg(lo7, [("I", R("sg")), ("B1", R("ind"))])
        act(R("dh"), lo7, RL, -1.0)
        cl, ch = R("cl_", 8, 264), R("ch_", 8, 264)
        ts(R("dl"), lo6, -1.0, A, 0.0, MX)
        sc(cl, R("dl"), R("c48"), 0.0, A, MN)
        sc(ch, R("dh"), R("c48"), 0.0, A, MN)
        for s in range(4):
            act(R("oh", 256 * s, 256 * s + 256), cl if s < 3 else ch, SG, R("mc", s % 3, s % 3 + 1), -1.0, R("acc", s, s + 1))
        for s, n in ((1, "jk"), (2, "jl")):
            ts(R(n, 0, 256), ch, R("mc", s, s + 1), LT, 2.0, MU)
        for s, n in ((4, "jk"), (5, "jl")):
            add("V", (lambda s, n: lambda: g.vector.tensor_reduce(R("acc", s, s + 1)[0], R(n)[0], AxisListType.X, A))(s, n),
                [R("acc", s, s + 1)], [R(n)])
        cU = R("cU", 0, 6)
        ts(cU, R("acc", 0, 6), 0.5, MU, 128.0, A)
        b1, b2 = 96 * t, 192 * t
        m1, l1 = R("m1", b1, b1 + 96), R("l1", b1, b1 + 96)
        ts(m1, X(R("tw"), cU), o7, A)
        send("m1", "l1", b1, 48, "r%d" % (3 * t))
        cp(R("fT"), X(R("Fa"), cU))
        act(R("r1"), lo5, RL, -240.0)
        act(R("r2"), R("r1"), RL, 126.0, -1.0)
        act(R("i256"), m1, RL, -256.0 * (4095 + o7), 256.0)
        mg(R("p7", 0, 96), [("W1", R("fT"))])
        mg(R("p7", 96, 192), [("W2", R("fT"))])
        act(R("m2", b2, b2 + 48), R("fT", 0, 48), CO)
        act(R("m2", b2 + 144, b2 + 192), R("fT", 48, 96), CO)
        act(R("Ns", 0, 48), R("m1", b1, b1 + 48), ID, 128.0 * (-2047 - o7) + 32, 128.0)
        act(R("Ns", 48, 96), R("m1", b1 + 48, b1 + 96), ID, 128.0 * (2049 - o7) + 32, 128.0)
        act(R("clF", 0, 6), R("acc", 0, 6), ID, 128.0, 0.5)
        act(R("t6", 0, 6), R("acc", 0, 6), RL, -127.0, 0.5)
        if t == 0:
            silu((6, 7))
        mg(hi5, [("nI", R("zb")), ("B1", R("c16")), ("nI", R("r2"))])
        cp(R("ui"), R("p7", 0, 192))
        ts(R("ui"), R("ui"), 4095, AN)
        tt(R("qi"), R("ui", 0, 96), R("ui", 96, 192), MU)
        ts(R("qi"), R("qi"), 5, SH, 255, AN)
        tt(R("m2", b2 + 48, b2 + 144), R("qi"), R("i256"), MX)
        send("m2", "l2", b2, 96, "r%d" % (3 * t + 1))
        dS = R("p6", 0, 96)
        tt(W, hi5, W, A)
        act(R("CS"), X(Wg, cU), CO)
        for i, (l, r) in enumerate([("BI", cl), ("nBI", R("cl_", 7, 263)), ("BI", ch), ("nBI", R("ch_", 7, 263))]):
            mm(lo4, R(l), r, i == 0, False)
        for h in range(4):
            mm(R("pd", 512 * h, 512 * h + 384), R("Z0"), R("D", 0, 384), True, False)
        tt(R("bd", 0, 6), R("t6", 0, 6), R("dum", 0, 6), MU)
        sc(R("sN"), R("dN"), l1, 0.0, A, MN)
        nU, aU, qU = R("U", 18, 24), R("U", 6, 12), R("U", 12, 18)
        tt(R("t6", 0, 6), R("bd", 0, 6), R("clF", 0, 6), MX)
        ts(nU, R("sN", 15, 96, 16), C(9), A, -o7, A)
        act(R("Nq"), l1, ID, 128.0 * (1 - o7) + 32, 128.0)
        cp(R("sU", 0, 6), R("t6", 0, 6))
        tt(R("gA"), X(R("inv", 0, 4104), nU), R("dg"), MU)
        tt(R("CT"), X(R("th"), cU), R("CS"), MU)
        sc(R("sA"), R("r0"), R("gA"), 0.0, MU, A)
        ts(R("a1", 0, 6), R("sA", 15, 96, 16), -31.0, A)
        ts(aU, R("sA", 15, 96, 16), -32.0, A)
        act(R("CC", 0, 96), X(Wg, aU), CO)

        def hot(j, src, col):
            s = j % 6
            o = R("oh", 256 * j, 256 * j + 256)
            ts(o, src, col, EQ, R("ww", 16 * s + 15, 16 * s + 16), MU)
            mm(lo4, R("B1"), o, False, j == 11)

        def minus_f(h):
            for u in range(512 * h, 512 * h + 384, 96):
                mm(R("pd", u, u + 48), R("nI"), R("l2", b2, b2 + 48), False, False)
                mm(R("pd", u + 48, u + 96), R("nI"), R("l2", b2 + 144, b2 + 192), False, False)

        for s in range(6):
            hot(s, R("iB", 1, 257), R("a1", s, s + 1))
        tt(R("eq"), X(R("y"), aU), l1, EQ)
        pA_, pB = R("p7", 0, 96), R("p5", 0, 192)
        mg(pA_, [("UmI", R("CC", 0, 96))])
        mg(R("p5", 0, 96), [("TRI", R("eq"))])
        qr = R("l2", b2 + 48, b2 + 144)
        ts(R("oQ"), qr, 16.0, MU, C(3), A)
        tt(R("qd"), qr, R("dg"), MU)
        act(R("Fq"), X(Fw, R("oQ")), CO)
        act(R("ge"), R("p5", 0, 96), CO)
        sc(R("sQ"), R("r0"), R("qd"), 0.0, MU, A)
        minus_f(0)
        minus_f(1)
        for s in range(6):
            hot(6 + s, R("iB", 0, 256), R("sQ", 16 * s + 15, 16 * s + 16))
        minus_f(2)
        minus_f(3)
        ts(R("U", 0, 6), R("sQ", 15, 96, 16), 264.0, A)
        cp(qU, R("sQ", 15, 96, 16))
        act(R("kb"), X(R("va"), qU), ID, C(11), -8192.0)
        for k in range(16):
            u = 512 * (k // 4) + 96 * (k % 4)
            mm(R("pd", u, u + 96), R("I"), R("Fq", k, 1536, 16), False, k % 4 == 3)
        for h in range(4):
            act(R("Ab", 384 * h, 384 * h + 384), R("pd", 512 * h, 512 * h + 384), AF.Abs)
        tt(R("Tt", 0, 256), lo4, R("pA"), A)
        tt(R("Tt", 264, 520), lo4, R("pQ"), A)
        tt(R("lt"), X(R("Tt"), R("U", 0, 12)), R("thr"), LT)
        cp(R("CC", 96, 192), X(Wg, qU))
        gd = R("gd", b1, b1 + 96)
        tt(gd, R("lt", 0, 96), R("lt", 96, 192), MU)
        send("gd", "la", b1, 48, "r%d" % (3 * t + 2), True)
        CQ = R("CC", 96, 192)
        K = R("p4", 0, 96)
        mm(K, R("I32"), R("kb"), True, False)
        mg(R("p5", 0, 96), [("I32", R("Nq")), ("nDn32", CQ)])
        for k in range(16):
            mm(K, R("Z", 15 - k, 143 - k), R("Ab", 96 * k, 96 * k + 96), False, k == 15)
        mg(dS, [("Dn32", R("CS")), ("nI32", R("CS")), ("nDq", R("CT")), ("E0", R("Ns"))])
        mg(R("p5", 96, 192), [("Dn32", CQ), ("nI32", CQ)])
        tt(R("bad"), gd, R("dg"), LT)
        cp(R("OF", 0, 18), R("U", 6, 24))
        sc(R("sB"), R("r0"), R("bad"), 0.0, MU, A)
        tt(R("XX", 0, 96), pA_, R("ge"), MU)
        tt(R("bd"), X(R("sB"), R("eL")), R("dum"), MU)
        tt(R("of2"), R("bd"), R("OF"), MX)
        cp(R("fU", 0, 18), R("of2", 0, 18))
        tt(X(R("W"), R("fU", 0, 6)), R("XX", 0, 96), R("CC", 0, 96), A)
        if not last:
            act(R("q32"), qr, ID, 32.0)
            act(X(R("inv"), R("fU", 12, 18)), R("q32"), AF.Silu)
        if t == 0:
            scaled((("M1", "Dn", -77.0 / 64), ("M2", "Dn", -154.0 / 64), ("M3", "Dn", -231.0 / 64)))
        tr(R("KP", 0, 96), K)
        sc(R("KP", 96, 192), R("rB"), R("KP", 0, 96), 0.0, A, MN)
        tt(R("mT", 0, 96), X(R("KP", 96, 192), R("aL")), R("KP", 0, 96), EQ)
        tt(R("XS"), dS, R("la", b1, b1 + 96), MU)
        sc(R("mT", 96, 192), R("r0"), R("mT", 0, 96), 0.0, MU, A)
        tt(X(R("W"), R("sU", 0, 6)), R("XS"), R("CS"), A)
        tr(R("mk"), R("mT"))
        tt(R("PP"), pB, R("mk"), MU)
        tt(R("XX", 96, 192), R("PP", 0, 96), R("PP", 96, 192), A)
        tt(X(R("W"), R("fU", 6, 12)), R("XX", 96, 192), CQ, A)
    cp(R("Wi"), W)
    act(va, W, SG)
    mm(R("p6", 0, 256, 1, 8), R("B1", 0, 128, 16), va)
    act(R("yn_", 0, 256, 1, 8), R("p6", 0, 256, 1, 8), CO)
    ts(R("xm"), R("Wi"), 7, SH)
    ts(R("z2"), R("Wi"), 1, SH, 63, AN)
    ts(R("yl_"), R("xm"), -1.0, A)
    cp(R("yz_"), R("z2"))
    dma("S", T.yn[:], R("yn_", 0, 256, 1, 8))
    dma("Y", T.yl[:], R("yl_"))
    dma("S", T.yz[:], R("yz_"))

    hist = {}
    deps = []
    for i, (e, fn, rd, wr, sem) in enumerate(ops):
        best = {}
        for regs, w in ((rd, False), (wr, True)):
            for n, lo, hi in regs:
                for lo2, hi2, j, w2 in hist.get(n, ()):
                    if lo < hi2 and lo2 < hi:
                        same = ops[j][0] == e and ops[j][4] is None
                        if (w or w2 or (n in _P and not same)) and not (same and e == "P") and e != "X" and ops[j][4] != ("", 0):
                            key = ops[j][4][0] if ops[j][4] else ops[j][0]
                            best[key] = max(best.get(key, -1), j)
        for regs, w in ((rd, False), (wr, True)):
            for n, lo, hi in regs:
                h = hist.setdefault(n, [])
                if w:
                    h[:] = [x for x in h if not (lo <= x[0] and x[1] <= hi)]
                h.append((lo, hi, i, w))
        deps.append(best)
    seen = {}
    need = set()
    for i, o in enumerate(ops):
        for key in list(deps[i]):
            if seen.get((o[0], key), -1) >= deps[i][key]:
                del deps[i][key]
            else:
                seen[(o[0], key)] = deps[i][key]
                need.add(deps[i][key])
    val = {}
    n = {}
    for i, (e, fn, rd, wr, sem) in enumerate(ops):
        if sem:
            val[i] = sem
        elif i in need:
            n[e] = n.get(e, 0) + 1
            val[i] = ("e" + e, n[e])
        if e == "X":
            continue
        for key, j in deps[i].items():
            Q[e].wait_ge(T.sem[val[j][0]], val[j][1])
        r = fn()
        if sem and sem[0]:
            r.then_inc(T.sem[sem[0]], 16)
        elif not sem and i in need:
            r.then_inc(T.sem["e" + e], 1)
    g.wait_ge(T.sem.loc, nloc[0])
    for i in range(nd[0] - 3, nd[0]):
        g.sync.wait_ge(T.sem["d%d" % i], 16)
